import numpy as np
import ml_dtypes


def mxq(x, axis, fmt="e4m3"):
    dtype, down = {"e4m3": (ml_dtypes.float8_e4m3fn, 7), "e5m2": (ml_dtypes.float8_e5m2, 14)}[fmt]
    v = np.moveaxis(np.asarray(x, np.float32).astype(ml_dtypes.bfloat16).astype(np.float64), axis, -1)
    blocks = v.reshape(v.shape[:-1] + (-1, 32))
    amax = np.abs(blocks).max(-1, keepdims=True)
    byte = np.maximum(np.where(amax > 0, np.frexp(amax)[1] - 1 + 127, 0) - down, 1)
    scale = np.exp2(byte - 127.0)
    codes = (blocks / scale).astype(np.float32).astype(dtype).astype(np.float64)
    return np.moveaxis((codes * scale).reshape(v.shape), -1, axis)


WIDE = False


def mx_kscale(k):
    if not WIDE:
        return np.ones(k)
    levels = np.array([10, -10, 5, -5, 0])
    if k % 512:
        return np.exp2(np.random.permutation(np.resize(levels, k // 32))).repeat(32)
    a = np.empty((k // 512, 16))
    for p in range(k // 512):
        a[p, :8] = np.random.permutation(np.resize(levels, 8))
        for g in range(8):
            far = levels[np.abs(levels - a[p, g]) >= 10]
            a[p, g + 8] = far[np.random.randint(len(far))]
    return np.exp2(a.ravel()).repeat(32)


def f64(x):
    return np.asarray(x).astype(np.float64)


E2M1 = np.array([0.0, 0.5, 1.0, 1.5, 2.0, 3.0, 4.0, 6.0, -0.0, -0.5, -1.0, -1.5, -2.0, -3.0, -4.0, -6.0])


def pack_weight(w, fmt):
    k, n = w.shape
    w = f64(np.asarray(w, np.float32).astype(ml_dtypes.bfloat16)).reshape(k // 32, 32, n)
    amax = np.abs(w).max(1)
    if fmt == "e4m3":
        byte = np.frexp(amax)[1] - 1 + 127 - 7
    else:
        mant, ex = np.frexp(amax / 6.0)
        byte = np.where(mant > 0.5, ex, ex - 1) + 127
    byte = np.clip(np.where(amax > 0, byte, 1), 1, 254)
    scaled = (w * np.exp2(127.0 - byte)[:, None, :]).reshape(k, n).astype(np.float32)
    by_word = np.ascontiguousarray(scaled.reshape(k // 512, 128, 4, n).transpose(0, 1, 3, 2))
    if fmt == "e4m3":
        words = by_word.astype(ml_dtypes.float8_e4m3fn).view(np.uint8)
    else:
        c = by_word.astype(ml_dtypes.float4_e2m1fn).view(np.uint8) & 0xF
        words = (c[..., 0::2] | (c[..., 1::2] << 4)).reshape(k // 512, 128, 2 * n)
    return np.ascontiguousarray(words), np.ascontiguousarray(byte.astype(np.uint8).reshape(k // 512, 16, n))


def unpack_weight(words, scales, fmt):
    g, _, n = scales.shape
    words = np.ascontiguousarray(words).reshape(g, 128, n, -1)
    if fmt == "e4m3":
        vals = words.view(ml_dtypes.float8_e4m3fn).astype(np.float64)
    else:
        nib = np.empty((g, 128, n, 4), np.uint8)
        nib[..., 0::2] = words & 0xF
        nib[..., 1::2] = words >> 4
        vals = E2M1[nib]
    vals = vals * np.repeat(np.exp2(scales.astype(np.float64) - 127.0), 8, axis=1)[..., None]
    return vals.transpose(0, 1, 3, 2).reshape(g * 512, n)


def bf(x):
    return np.asarray(x, np.float32).astype(ml_dtypes.bfloat16)


def planes(Y):
    r, m = Y.shape
    b = f64(bf(Y)).reshape(r // 32, 32, m)
    amax = np.abs(b).max(1)
    byte = np.clip(np.where(amax > 0, np.frexp(amax)[1] - 1 + 127 - 7, 1), 1, 254)
    codes = (b * np.exp2(127.0 - byte)[:, None, :]).reshape(r, m).astype(np.float32).astype(ml_dtypes.float8_e4m3fn).view(np.uint8)
    words = codes.reshape(r // 512, 128, 4, m).transpose(0, 1, 3, 2)
    return np.ascontiguousarray(words), np.ascontiguousarray(byte.astype(np.uint8).reshape(r // 512, 16, m))


K, L, T, N = 1024, 1024, 512, 512


def setup_inputs():
    n = np.random.standard_normal
    fk = mx_kscale(K)
    fl = mx_kscale(L)
    xtp = pack_weight(n((K, T)) / fk[:, None], "e2m1")
    xqp = pack_weight(n((L, T)) / fl[:, None], "e4m3")
    wqp = pack_weight(n((L, N)) * 1 / np.sqrt(L) * fl[:, None], "e2m1")
    return {
        "xt_words": xtp[0],
        "xt_scales": xtp[1],
        "ea": (n((K, N)) * 1 / np.sqrt(K) * fk[:, None]).astype(np.float32),
        "eb": (n((K, N)) * 1 / np.sqrt(K) * fk[:, None]).astype(np.float32),
        "sh": (np.random.uniform(0.2, 0.8, (1, N))).astype(np.float32),
        "xq_words": xqp[0],
        "xq_scales": xqp[1],
        "wq_words": wqp[0],
        "wq_scales": wqp[1],
    }


def reference(xt_words, xt_scales, ea, eb, sh, xq_words, xq_scales, wq_words, wq_scales):
    xtu = unpack_weight(xt_words, xt_scales, "e2m1")
    xqu = unpack_weight(xq_words, xq_scales, "e4m3")
    wqu = unpack_weight(wq_words, wq_scales, "e2m1")
    em = f64(eb) + f64(sh) * (f64(ea) - f64(eb))
    emq = mxq(em, 0, "e4m3")
    y = emq.T @ xtu + wqu.T @ xqu
    words, scales = planes(y)
    return y, words, scales

@@ -1,0 +1,278 @@
+from contextlib import ExitStack
+
+import concourse.mybir as mybir
+from concourse.masks import make_identity
+
+K, L, T, N = 1024, 1024, 512, 512
+FLOPS = 2 * (K + L) * T * N
+
+F32 = mybir.dt.float32
+BF16 = mybir.dt.bfloat16
+I32 = mybir.dt.int32
+U32 = mybir.dt.uint32
+U8 = mybir.dt.uint8
+FP8X4 = mybir.dt.float8_e4m3fn_x4
+FP4X4 = mybir.dt.float4_e2m1fn_x4
+ALU = mybir.AluOpType
+COPY = mybir.ActivationFunctionType.Copy
+
+P = 128
+
+
+def tile_mix_blended_weights_and_given_pl_kernel(
+    tc, xt_words, xt_scales, ea, eb, sh, xq_words, xq_scales, wq_words, wq_scales, out_0, out_1, out_2
+):
+    nc = tc.nc
+    with ExitStack() as ctx:
+        keep = ctx.enter_context(tc.tile_pool(name="keep", bufs=1))
+        psum = ctx.enter_context(tc.psum_pool(name="psum", bufs=1))
+        ctx.enter_context(tc.manual_schedule())
+
+        def sb(name, shape, dtype):
+            return keep.tile(shape, dtype, name=name, align_bytes=64)
+
+        def bank(i, name):
+            return psum.tile([P, 512], F32, name=name, tag="bank%d" % i)
+
+        ident = sb("ident", [P, P], F32)
+        sh_col = sb("sh_col", [P, 4], F32)
+        rest_col = sb("rest_col", [P, 4], F32)
+        warm_in = sb("warm_in", [P, 1], F32)
+        warm_out = sb("warm_out", [P, 1], F32)
+        ws_raw = sb("ws_raw", [P, 1024], U8)
+        xq_s = sb("xq_s", [P, 1024], U8)
+        xt_s = sb("xt_s", [P, 1024], U8)
+        wq_raw = sb("wq_raw", [P, 2048], U8)
+        wq_w = [sb("wq_w%d" % g, [P, 1024], U8) for g in range(2)]
+        wq_s = [sb("wq_s%d" % g, [P, 512], U8) for g in range(2)]
+        xq_w = [sb("xq_w%d" % g, [P, 2048], U8) for g in range(2)]
+        xt_w = [sb("xt_w%d" % g, [P, 1024], U8) for g in range(2)]
+        em_w = [sb("em_w%d" % g, [P, 512], U32) for g in range(2)]
+        em_s = [sb("em_s%d" % g, [P, 512], U8) for g in range(2)]
+        grouped = [sb("grouped%d" % g, [P, 2048], BF16) for g in range(2)]
+
+        nc.vector.memset(ws_raw[:].bitcast(I32), 0)
+        nc.vector.memset(warm_in[:], 0.0)
+        nc.vector.memset(xq_s[:].bitcast(I32), 0)
+        nc.vector.memset(xt_s[:].bitcast(I32), 0)
+        nc.scalar.activation(out=warm_out[:], in_=warm_in[:], func=COPY)
+        make_identity(nc, ident[:])
+
+        raw = {}
+
+        def load_rows(which, src, g, u, h0, h1):
+            t = sb("raw_%s%d%d%d" % (which, g, u, h0), [P, 2, 256 * (h1 - h0)], F32)
+            rows = src[512 * g : 512 * (g + 1), :].rearrange("(p j) n -> p j n", j=4)
+            nc.sync.dma_start(out=t[:], in_=rows[:, 2 * u : 2 * u + 2, 256 * h0 : 256 * h1])
+            for h in range(h0, h1):
+                raw[which, g, u, h] = t[:, :, 256 * (h - h0) : 256 * (h - h0 + 1)]
+
+        def load_scales(dst, src):
+            rows = src.bitcast(I32).rearrange("g (q r) c -> r q g c", r=4)
+            view = dst[:].bitcast(I32).rearrange("p (g c) -> p g c", g=2)
+            for r in range(4):
+                nc.sync.dma_start(out=view[r:P:32], in_=rows[r])
+
+        load_rows("a", ea, 0, 0, 0, 2)
+        with nc.allow_non_contiguous_dma(reason="one share a partition"):
+            nc.sync.dma_start(out=sh_col[:], in_=sh.rearrange("o (b q) -> q (o b)", q=P))
+        load_scales(ws_raw, wq_scales)
+        nc.sync.dma_start(out=wq_raw[:].rearrange("p (g c) -> p g c", g=2), in_=wq_words.rearrange("g p c -> p g c"))
+        load_rows("b", eb, 0, 0, 0, 2)
+        nc.sync.dma_start(out=xq_w[0][:], in_=xq_words[0].rearrange("p c r -> p (c r)"))
+        load_scales(xq_s, xq_scales)
+        load_rows("a", ea, 0, 1, 0, 2)
+        load_rows("b", eb, 0, 1, 0, 2)
+        load_rows("a", ea, 1, 0, 0, 2)
+        load_rows("b", eb, 1, 0, 0, 2)
+        load_scales(xt_s, xt_scales)
+        nc.sync.dma_start(out=xt_w[0][:], in_=xt_words[0])
+        load_rows("a", ea, 1, 1, 0, 2)
+        load_rows("b", eb, 1, 1, 0, 1)
+        load_rows("b", eb, 1, 1, 1, 2)
+        nc.sync.dma_start(out=xq_w[1][:], in_=xq_words[1].rearrange("p c r -> p (c r)"))
+        nc.sync.dma_start(out=xt_w[1][:], in_=xt_words[1])
+
+        nc.vector.tensor_scalar(out=rest_col[:], in0=sh_col[:], scalar1=-1.0, scalar2=1.0, op0=ALU.mult, op1=ALU.add)
+
+        def deal_wq(g):
+            nc.vector.tensor_copy(
+                out=wq_w[g][:].rearrange("p (r m z) -> p r m z", r=4, z=2),
+                in_=wq_raw[:, 1024 * g : 1024 * (g + 1)].rearrange("p (m r z) -> p r m z", r=4, z=2),
+            )
+            nc.vector.tensor_copy(
+                out=wq_s[g][:].rearrange("p (r m) -> p r m", r=4),
+                in_=ws_raw[:, 512 * g : 512 * (g + 1)].rearrange("p (m r) -> p r m", r=4),
+            )
+
+        acc = [bank(4 + r, "acc%d" % r) for r in range(4)]
+        turned = {}
+        part = {}
+        emt = {}
+
+        def turn(which, g, u, h):
+            t = bank(h if which == "a" else 2 + h, "turned_%s%d%d%d" % (which, g, u, h))
+            turned[which, g, u, h] = t
+            for bb in range(2):
+                for e in range(2):
+                    c = 128 * (2 * bb + e)
+                    nc.tensor.transpose(t[:, c : c + 128], raw[which, g, u, h][:, e, 128 * bb : 128 * (bb + 1)], ident[:])
+
+        def pairs(t, bb):
+            return t[:, 256 * bb : 256 * (bb + 1)].rearrange("q (e p) -> q p e", e=2)
+
+        def scale_a(g, u, h):
+            for bb in range(2):
+                b = 2 * h + bb
+                t = sb("part%d%d%d" % (g, u, b), [P, 256], F32)
+                part[g, u, b] = t
+                nc.scalar.activation(
+                    out=t[:].rearrange("q (p e) -> q p e", e=2),
+                    in_=pairs(turned["a", g, u, h], bb),
+                    func=COPY,
+                    scale=sh_col[:, b : b + 1],
+                )
+
+        def blend(g, u, b):
+            t = sb("emt%d%d%d" % (g, u, b), [P, 256], BF16)
+            emt[g, u, b] = t
+            nc.vector.scalar_tensor_tensor(
+                out=t[:].rearrange("q (p e) -> q p e", e=2),
+                in0=pairs(turned["b", g, u, b // 2], b % 2),
+                scalar=rest_col[:, b : b + 1],
+                in1=part[g, u, b][:].rearrange("q (p e) -> q p e", e=2),
+                op0=ALU.mult,
+                op1=ALU.add,
+            )
+
+        def turn_back(g, b0, nb, i):
+            t = bank(i, "back%d%d" % (g, b0))
+            for bb in range(nb):
+                for u in range(2):
+                    c = 128 * (u * nb + bb)
+                    nc.tensor.transpose(t[:, c : c + 128], emt[g, u, b0 + bb][:].bitcast(F32), ident[:])
+            return t
+
+        def gather(t, g, b0, nb, on_scalar):
+            src = t[:, 0 : 256 * nb].rearrange("p (u m r) -> p r m u", u=2, r=4)
+            dst = grouped[g][:].bitcast(F32).rearrange("p (r m u) -> p r m u", r=4, u=2)[:, :, 32 * b0 : 32 * (b0 + nb), :]
+            if on_scalar:
+                nc.scalar.copy(out=dst, in_=src)
+            else:
+                nc.vector.tensor_copy(out=dst, in_=src)
+
+        def quantise_em(g, r0, nr):
+            nc.vector.quantize_mx(
+                out=em_w[g][:, 128 * r0 : 128 * (r0 + nr)].bitcast(FP8X4),
+                scales=em_s[g][:, 128 * r0 : 128 * (r0 + nr)],
+                in_=grouped[g][:, 512 * r0 : 512 * (r0 + nr)],
+            )
+
+        def mm_given(g, r, start):
+            nc.tensor.matmul_mx(
+                out=acc[r][:],
+                lhsT=wq_w[g][:, 256 * r : 256 * (r + 1)].bitcast(FP4X4),
+                lhsT_scale=wq_s[g][:, 128 * r : 128 * (r + 1)],
+                rhs=xq_w[g][:].bitcast(FP8X4),
+                rhs_scale=xq_s[:, 512 * g : 512 * (g + 1)],
+                start=start,
+                stop=False,
+            )
+
+        def mm_blend(g, r, stop):
+            nc.tensor.matmul_mx(
+                out=acc[r][:],
+                lhsT=em_w[g][:, 128 * r : 128 * (r + 1)].bitcast(FP8X4),
+                lhsT_scale=em_s[g][:, 128 * r : 128 * (r + 1)],
+                rhs=xt_w[g][:].bitcast(FP4X4),
+                rhs_scale=xt_s[:, 512 * g : 512 * (g + 1)],
+                start=False,
+                stop=stop,
+            )
+
+        def a_side(g, u):
+            for h in range(2):
+                turn("a", g, u, h)
+            for h in range(2):
+                scale_a(g, u, h)
+
+        def b_side(g, u):
+            for h in range(2):
+                turn("b", g, u, h)
+            for b in range(4):
+                blend(g, u, b)
+
+        deal_wq(0)
+        deal_wq(1)
+        a_side(0, 0)
+        b_side(0, 0)
+        mm_given(0, 0, True)
+        mm_given(0, 1, True)
+        a_side(0, 1)
+        mm_given(0, 2, True)
+        b_side(0, 1)
+        mm_given(0, 3, True)
+        back = turn_back(0, 0, 2, 2)
+        gather(back, 0, 0, 2, True)
+        a_side(1, 0)
+        back = turn_back(0, 2, 2, 3)
+        gather(back, 0, 2, 2, False)
+        quantise_em(0, 0, 4)
+        b_side(1, 0)
+        mm_blend(0, 0, False)
+        mm_blend(0, 1, False)
+        a_side(1, 1)
+        turn("b", 1, 1, 0)
+        blend(1, 1, 0)
+        blend(1, 1, 1)
+        mm_blend(0, 2, False)
+        turn("b", 1, 1, 1)
+        blend(1, 1, 2)
+        blend(1, 1, 3)
+        back = turn_back(1, 0, 1, 0)
+        gather(back, 1, 0, 1, True)
+        back = turn_back(1, 1, 1, 1)
+        gather(back, 1, 1, 1, True)
+        mm_blend(0, 3, False)
+        back = turn_back(1, 2, 1, 2)
+        gather(back, 1, 2, 1, True)
+        back = turn_back(1, 3, 1, 0)
+        gather(back, 1, 3, 1, False)
+        for r in range(4):
+            mm_given(1, r, False)
+        for r in range(4):
+            quantise_em(1, r, 1)
+        for r in range(4):
+            mm_blend(1, r, True)
+
+        y = sb("y", [P, 4, T], F32)
+        y_bf = [sb("y_bf%d" % h, [P, 1024], BF16) for h in range(2)]
+        y_w = sb("y_w", [P, T], U32)
+        y_s = sb("y_s", [P, T], U8)
+        out_rows = out_0.rearrange("(p r) t -> p r t", r=4)
+        for r in range(4):
+            if r % 2 == 0:
+                nc.scalar.copy(out=y[:, r, :], in_=acc[r][:])
+            else:
+                nc.vector.tensor_copy(out=y[:, r, :], in_=acc[r][:])
+                nc.sync.dma_start(out=out_rows[:, r - 1 : r + 1, :], in_=y[:, r - 1 : r + 1, :])
+
+        def weave(h, c0, c1, on_scalar):
+            dst = y_bf[h][:, 4 * c0 : 4 * c1].rearrange("p (c i r) -> p c r i", i=4, r=4)
+            src = y[:, :, 256 * h + c0 : 256 * h + c1].rearrange("p r (c i) -> p c r i", i=4)
+            if on_scalar:
+                nc.scalar.copy(out=dst, in_=src)
+            else:
+                nc.vector.tensor_copy(out=dst, in_=src)
+
+        weave(1, 0, 192, True)
+        weave(0, 0, 256, False)
+        weave(1, 192, 256, False)
+        words_out = out_1[0].rearrange("p c r -> p (c r)").bitcast(I32)
+        for h in range(2):
+            cols = slice(256 * h, 256 * (h + 1))
+            nc.vector.quantize_mx(out=y_w[:, cols].bitcast(FP8X4), scales=y_s[:, cols], in_=y_bf[h][:])
+            nc.sync.dma_start(out=words_out[:, cols], in_=y_w[:, cols].bitcast(I32))
+        for q in range(4):
+            queue = nc.sync if q % 2 == 0 else nc.scalar
+            queue.dma_start(out=out_2[0].bitcast(I32)[4 * q : 4 * q + 4, :], in_=y_s[:].bitcast(I32)[32 * q : 32 * q + 4, :])

@@ -51,6 +51,15 @@ def tile_mix_blended_weights_and_given_pl_kernel(
         em_s = [sb("em_s%d" % g, [P, 512], U8) for g in range(2)]
         grouped = [sb("grouped%d" % g, [P, 2048], BF16) for g in range(2)]
 
+        zeros = sb("zeros", [P, 512], BF16)
+        zero_w = sb("zero_w", [P, 128], U32)
+        zero_s = sb("zero_s", [P, 128], U8)
+        sh_row = sb("sh_row", [P, 128], F32)
+        rest_row = sb("rest_row", [P, 128], F32)
+        direct = [sb("direct%d" % g, [P, 512], BF16) for g in range(2)]
+
+        nc.gpsimd.memset(zeros[:].bitcast(I32), 0)
+        nc.vector.quantize_mx(out=zero_w[:].bitcast(FP8X4), scales=zero_s[:], in_=zeros[:])
         nc.vector.memset(ws_raw[:].bitcast(I32), 0)
         nc.vector.memset(warm_in[:], 0.0)
         nc.vector.memset(xq_s[:].bitcast(I32), 0)
@@ -83,6 +92,7 @@ def tile_mix_blended_weights_and_given_pl_kernel(
         load_scales(xq_s, xq_scales)
         load_rows("a", ea, 0, 1, 0, 2)
         load_rows("b", eb, 0, 1, 0, 2)
+        nc.sync.dma_start(out=xq_w[1][:], in_=xq_words[1].rearrange("p c r -> p (c r)"))
         load_rows("a", ea, 1, 0, 0, 2)
         load_rows("b", eb, 1, 0, 0, 2)
         load_scales(xt_s, xt_scales)
@@ -90,7 +100,6 @@ def tile_mix_blended_weights_and_given_pl_kernel(
         load_rows("a", ea, 1, 1, 0, 2)
         load_rows("b", eb, 1, 1, 0, 1)
         load_rows("b", eb, 1, 1, 1, 2)
-        nc.sync.dma_start(out=xq_w[1][:], in_=xq_words[1].rearrange("p c r -> p (c r)"))
         nc.sync.dma_start(out=xt_w[1][:], in_=xt_words[1])
 
         nc.vector.tensor_scalar(out=rest_col[:], in0=sh_col[:], scalar1=-1.0, scalar2=1.0, op0=ALU.mult, op1=ALU.add)
@@ -113,7 +122,7 @@ def tile_mix_blended_weights_and_given_pl_kernel(
         def turn(which, g, u, h):
             t = bank(h if which == "a" else 2 + h, "turned_%s%d%d%d" % (which, g, u, h))
             turned[which, g, u, h] = t
-            for bb in range(2):
+            for bb in range(2 - h):
                 for e in range(2):
                     c = 128 * (2 * bb + e)
                     nc.tensor.transpose(t[:, c : c + 128], raw[which, g, u, h][:, e, 128 * bb : 128 * (bb + 1)], ident[:])
@@ -121,16 +130,54 @@ def tile_mix_blended_weights_and_given_pl_kernel(
         def pairs(t, bb):
             return t[:, 256 * bb : 256 * (bb + 1)].rearrange("q (e p) -> q p e", e=2)
 
-        def scale_a(g, u, h):
-            for bb in range(2):
-                b = 2 * h + bb
-                t = sb("part%d%d%d" % (g, u, b), [P, 256], F32)
-                part[g, u, b] = t
-                nc.scalar.activation(
-                    out=t[:].rearrange("q (p e) -> q p e", e=2),
-                    in_=pairs(turned["a", g, u, h], bb),
-                    func=COPY,
-                    scale=sh_col[:, b : b + 1],
+        def scale_a(g, u, b):
+            t = sb("part%d%d%d" % (g, u, b), [P, 256], F32)
+            part[g, u, b] = t
+            nc.scalar.activation(
+                out=t[:].rearrange("q (p e) -> q p e", e=2),
+                in_=pairs(turned["a", g, u, b // 2], b % 2),
+                func=COPY,
+                scale=sh_col[:, b : b + 1],
+            )
+
+        prod = {}
+
+        def direct_mul(which, g, u):
+            t = sb("prod_%s%d%d" % (which, g, u), [P, 2, 128], F32)
+            prod[which, g, u] = t
+            row = sh_row if which == "a" else rest_row
+            nc.gpsimd.tensor_tensor(
+                out=t[:],
+                in0=raw[which, g, u, 1][:, :, 128:256],
+                in1=row[:].unsqueeze(1).broadcast_to([P, 2, 128]),
+                op=ALU.mult,
+            )
+
+        def direct_add(g, u):
+            engine = nc.vector if (g, u) == (1, 1) else nc.gpsimd
+            engine.tensor_tensor(
+                out=direct[g][:, 256 * u : 256 * (u + 1)],
+                in0=prod["a", g, u][:].rearrange("p e n -> p (e n)"),
+                in1=prod["b", g, u][:].rearrange("p e n -> p (e n)"),
+                op=ALU.add,
+            )
+
+        def direct_gather(g):
+            nc.vector.tensor_copy(
+                out=grouped[g][:].rearrange("p (r m j) -> p r m j", r=4, j=4)[:, :, 96:128, :],
+                in_=direct[g][:].rearrange("p (j m r) -> p r m j", j=4, r=4),
+            )
+
+        def warm(count):
+            for i in range(count):
+                nc.tensor.matmul_mx(
+                    out=acc[3][:, 0:128],
+                    lhsT=zero_w[:].bitcast(FP8X4),
+                    lhsT_scale=zero_s[:],
+                    rhs=zero_w[:].bitcast(U8)[:, 0:256].bitcast(FP4X4),
+                    rhs_scale=zero_s[:],
+                    start=True,
+                    stop=True,
                 )
 
         def blend(g, u, b):
@@ -190,45 +237,71 @@ def tile_mix_blended_weights_and_given_pl_kernel(
                 stop=stop,
             )
 
+        def turn_both(which, g, u):
+            for h in range(2):
+                turn(which, g, u, h)
+
         def a_side(g, u):
-            for h in range(2):
-                turn("a", g, u, h)
-            for h in range(2):
-                scale_a(g, u, h)
+            turn_both("a", g, u)
+            for b in range(3):
+                scale_a(g, u, b)
+            direct_mul("a", g, u)
 
         def b_side(g, u):
-            for h in range(2):
-                turn("b", g, u, h)
-            for b in range(4):
+            turn_both("b", g, u)
+            direct_mul("b", g, u)
+            for b in range(3):
                 blend(g, u, b)
+            direct_add(g, u)
 
+        warm(18)
+        spread = bank(3, "spread")
+        nc.tensor.transpose(spread[:, 0:128], sh_col[:, 3:4].to_broadcast([P, P]), ident[:])
+        nc.vector.tensor_copy(out=sh_row[:], in_=spread[:, 0:128])
+        nc.vector.tensor_scalar(out=rest_row[:], in0=spread[:, 0:128], scalar1=-1.0, scalar2=1.0, op0=ALU.mult, op1=ALU.add)
+        a_side(0, 0)
+        warm(8)
         deal_wq(0)
         deal_wq(1)
-        a_side(0, 0)
         b_side(0, 0)
         mm_given(0, 0, True)
         mm_given(0, 1, True)
         a_side(0, 1)
         mm_given(0, 2, True)
-        b_side(0, 1)
         mm_given(0, 3, True)
+        b_side(0, 1)
+        mm_given(1, 0, False)
+        mm_given(1, 1, False)
         back = turn_back(0, 0, 2, 2)
         gather(back, 0, 0, 2, True)
-        a_side(1, 0)
-        back = turn_back(0, 2, 2, 3)
-        gather(back, 0, 2, 2, False)
+        turn_both("a", 1, 0)
+        scale_a(1, 0, 0)
+        direct_mul("a", 1, 0)
+        direct_gather(0)
+        back = turn_back(0, 2, 1, 3)
+        gather(back, 0, 2, 1, True)
+        scale_a(1, 0, 1)
+        scale_a(1, 0, 2)
+        mm_given(1, 2, False)
+        mm_given(1, 3, False)
+        turn_both("b", 1, 0)
+        direct_mul("b", 1, 0)
         quantise_em(0, 0, 4)
-        b_side(1, 0)
+        for b in range(3):
+            blend(1, 0, b)
+        direct_add(1, 0)
         mm_blend(0, 0, False)
         mm_blend(0, 1, False)
         a_side(1, 1)
         turn("b", 1, 1, 0)
         blend(1, 1, 0)
-        blend(1, 1, 1)
         mm_blend(0, 2, False)
         turn("b", 1, 1, 1)
+        direct_mul("b", 1, 1)
+        blend(1, 1, 1)
         blend(1, 1, 2)
-        blend(1, 1, 3)
+        direct_add(1, 1)
+        direct_gather(1)
         back = turn_back(1, 0, 1, 0)
         gather(back, 1, 0, 1, True)
         back = turn_back(1, 1, 1, 1)
@@ -236,10 +309,6 @@ def tile_mix_blended_weights_and_given_pl_kernel(
         mm_blend(0, 3, False)
         back = turn_back(1, 2, 1, 2)
         gather(back, 1, 2, 1, True)
-        back = turn_back(1, 3, 1, 0)
-        gather(back, 1, 3, 1, False)
-        for r in range(4):
-            mm_given(1, r, False)
         for r in range(4):
             quantise_em(1, r, 1)
         for r in range(4):
@@ -250,12 +319,13 @@ def tile_mix_blended_weights_and_given_pl_kernel(
         y_w = sb("y_w", [P, T], U32)
         y_s = sb("y_s", [P, T], U8)
         out_rows = out_0.rearrange("(p r) t -> p r t", r=4)
-        for r in range(4):
-            if r % 2 == 0:
-                nc.scalar.copy(out=y[:, r, :], in_=acc[r][:])
-            else:
-                nc.vector.tensor_copy(out=y[:, r, :], in_=acc[r][:])
-                nc.sync.dma_start(out=out_rows[:, r - 1 : r + 1, :], in_=y[:, r - 1 : r + 1, :])
+        nc.vector.tensor_copy(out=y[:, 0, :], in_=acc[0][:])
+        nc.scalar.copy(out=y[:, 1, :], in_=acc[1][:])
+        nc.sync.dma_start(out=out_rows[:, 0:2, :], in_=y[:, 0:2, :])
+        nc.vector.tensor_copy(out=y[:, 2, :], in_=acc[2][:])
+        nc.scalar.copy(out=y[:, 3, 0:256], in_=acc[3][:, 0:256])
+        nc.scalar.copy(out=y[:, 3, 256:512], in_=acc[3][:, 256:512])
+        nc.sync.dma_start(out=out_rows[:, 2:4, :], in_=y[:, 2:4, :])
 
         def weave(h, c0, c1, on_scalar):
             dst = y_bf[h][:, 4 * c0 : 4 * c1].rearrange("p (c i r) -> p c r i", i=4, r=4)
@@ -265,9 +335,9 @@ def tile_mix_blended_weights_and_given_pl_kernel(
             else:
                 nc.vector.tensor_copy(out=dst, in_=src)
 
-        weave(1, 0, 192, True)
         weave(0, 0, 256, False)
-        weave(1, 192, 256, False)
+        weave(1, 0, 128, True)
+        weave(1, 128, 256, False)
         words_out = out_1[0].rearrange("p c r -> p (c r)").bitcast(I32)
         for h in range(2):
             cols = slice(256 * h, 256 * (h + 1))

@@ -54,16 +54,19 @@ def tile_mix_blended_weights_and_given_pl_kernel(
         zeros = sb("zeros", [P, 512], BF16)
         zero_w = sb("zero_w", [P, 128], U32)
         zero_s = sb("zero_s", [P, 128], U8)
+        sh_rows = sb("sh_rows", [P, 128], F32)
         sh_row = sb("sh_row", [P, 128], F32)
         rest_row = sb("rest_row", [P, 128], F32)
         direct = [sb("direct%d" % g, [P, 512], BF16) for g in range(2)]
 
-        nc.gpsimd.memset(zeros[:].bitcast(I32), 0)
-        nc.vector.quantize_mx(out=zero_w[:].bitcast(FP8X4), scales=zero_s[:], in_=zeros[:])
-        nc.vector.memset(ws_raw[:].bitcast(I32), 0)
+        nc.gpsimd.memset(sh_rows[:], 0.0)
+        nc.gpsimd.memset(ws_raw[:].bitcast(I32), 0)
+        nc.vector.memset(zeros[:].bitcast(I32), 0)
         nc.vector.memset(warm_in[:], 0.0)
+        nc.vector.quantize_mx(out=zero_w[:].bitcast(FP8X4), scales=zero_s[:], in_=zeros[:])
         nc.vector.memset(xq_s[:].bitcast(I32), 0)
         nc.vector.memset(xt_s[:].bitcast(I32), 0)
+        nc.scalar.dma_start(out=sh_rows[0:4, :], in_=sh.rearrange("o (b q) -> (o b) q", q=P))
         nc.scalar.activation(out=warm_out[:], in_=warm_in[:], func=COPY)
         make_identity(nc, ident[:])
 
@@ -76,39 +79,37 @@ def tile_mix_blended_weights_and_given_pl_kernel(
             for h in range(h0, h1):
                 raw[which, g, u, h] = t[:, :, 256 * (h - h0) : 256 * (h - h0 + 1)]
 
-        def load_scales(dst, src):
+        def load_scales(queue, dst, src):
             rows = src.bitcast(I32).rearrange("g (q r) c -> r q g c", r=4)
             view = dst[:].bitcast(I32).rearrange("p (g c) -> p g c", g=2)
             for r in range(4):
-                nc.sync.dma_start(out=view[r:P:32], in_=rows[r])
+                queue.dma_start(out=view[r:P:32], in_=rows[r])
 
         load_rows("a", ea, 0, 0, 0, 2)
-        with nc.allow_non_contiguous_dma(reason="one share a partition"):
-            nc.sync.dma_start(out=sh_col[:], in_=sh.rearrange("o (b q) -> q (o b)", q=P))
-        load_scales(ws_raw, wq_scales)
+        load_scales(nc.sync, ws_raw, wq_scales)
         nc.sync.dma_start(out=wq_raw[:].rearrange("p (g c) -> p g c", g=2), in_=wq_words.rearrange("g p c -> p g c"))
         load_rows("b", eb, 0, 0, 0, 2)
         nc.sync.dma_start(out=xq_w[0][:], in_=xq_words[0].rearrange("p c r -> p (c r)"))
-        load_scales(xq_s, xq_scales)
+        load_scales(nc.sync, xq_s, xq_scales)
         load_rows("a", ea, 0, 1, 0, 2)
         load_rows("b", eb, 0, 1, 0, 2)
-        nc.sync.dma_start(out=xq_w[1][:], in_=xq_words[1].rearrange("p c r -> p (c r)"))
         load_rows("a", ea, 1, 0, 0, 2)
         load_rows("b", eb, 1, 0, 0, 2)
-        load_scales(xt_s, xt_scales)
+        load_scales(nc.sync, xt_s, xt_scales)
         nc.sync.dma_start(out=xt_w[0][:], in_=xt_words[0])
         load_rows("a", ea, 1, 1, 0, 2)
         load_rows("b", eb, 1, 1, 0, 1)
         load_rows("b", eb, 1, 1, 1, 2)
+        nc.sync.dma_start(out=xq_w[1][:], in_=xq_words[1].rearrange("p c r -> p (c r)"))
         nc.sync.dma_start(out=xt_w[1][:], in_=xt_words[1])
 
-        nc.vector.tensor_scalar(out=rest_col[:], in0=sh_col[:], scalar1=-1.0, scalar2=1.0, op0=ALU.mult, op1=ALU.add)
-
-        def deal_wq(g):
+        def deal_words(g):
             nc.vector.tensor_copy(
                 out=wq_w[g][:].rearrange("p (r m z) -> p r m z", r=4, z=2),
                 in_=wq_raw[:, 1024 * g : 1024 * (g + 1)].rearrange("p (m r z) -> p r m z", r=4, z=2),
             )
+
+        def deal_scales(g):
             nc.vector.tensor_copy(
                 out=wq_s[g][:].rearrange("p (r m) -> p r m", r=4),
                 in_=ws_raw[:, 512 * g : 512 * (g + 1)].rearrange("p (m r) -> p r m", r=4),
@@ -146,7 +147,8 @@ def tile_mix_blended_weights_and_given_pl_kernel(
             t = sb("prod_%s%d%d" % (which, g, u), [P, 2, 128], F32)
             prod[which, g, u] = t
             row = sh_row if which == "a" else rest_row
-            nc.gpsimd.tensor_tensor(
+            engine = nc.vector if (which, g, u) == ("a", 0, 0) else nc.gpsimd
+            engine.tensor_tensor(
                 out=t[:],
                 in0=raw[which, g, u, 1][:, :, 128:256],
                 in1=row[:].unsqueeze(1).broadcast_to([P, 2, 128]),
@@ -254,61 +256,58 @@ def tile_mix_blended_weights_and_given_pl_kernel(
                 blend(g, u, b)
             direct_add(g, u)
 
-        warm(18)
+        warm(12)
+        columns = bank(2, "columns")
+        nc.tensor.transpose(columns[:, 0:128], sh_rows[:], ident[:])
+        nc.vector.tensor_copy(out=sh_col[:], in_=columns[:, 0:4])
+        nc.vector.tensor_scalar(out=rest_col[:], in0=columns[:, 0:4], scalar1=-1.0, scalar2=1.0, op0=ALU.mult, op1=ALU.add)
+        warm(3)
         spread = bank(3, "spread")
         nc.tensor.transpose(spread[:, 0:128], sh_col[:, 3:4].to_broadcast([P, P]), ident[:])
         nc.vector.tensor_copy(out=sh_row[:], in_=spread[:, 0:128])
         nc.vector.tensor_scalar(out=rest_row[:], in0=spread[:, 0:128], scalar1=-1.0, scalar2=1.0, op0=ALU.mult, op1=ALU.add)
         a_side(0, 0)
         warm(8)
-        deal_wq(0)
-        deal_wq(1)
+        deal_words(0)
+        deal_scales(0)
+        deal_words(1)
+        deal_scales(1)
         b_side(0, 0)
         mm_given(0, 0, True)
         mm_given(0, 1, True)
         a_side(0, 1)
         mm_given(0, 2, True)
-        mm_given(0, 3, True)
         b_side(0, 1)
-        mm_given(1, 0, False)
-        mm_given(1, 1, False)
+        mm_given(0, 3, True)
         back = turn_back(0, 0, 2, 2)
         gather(back, 0, 0, 2, True)
         turn_both("a", 1, 0)
-        scale_a(1, 0, 0)
-        direct_mul("a", 1, 0)
-        direct_gather(0)
         back = turn_back(0, 2, 1, 3)
         gather(back, 0, 2, 1, True)
-        scale_a(1, 0, 1)
-        scale_a(1, 0, 2)
-        mm_given(1, 2, False)
-        mm_given(1, 3, False)
-        turn_both("b", 1, 0)
-        direct_mul("b", 1, 0)
+        direct_gather(0)
         quantise_em(0, 0, 4)
         for b in range(3):
-            blend(1, 0, b)
-        direct_add(1, 0)
+            scale_a(1, 0, b)
+        direct_mul("a", 1, 0)
+        b_side(1, 0)
         mm_blend(0, 0, False)
         mm_blend(0, 1, False)
         a_side(1, 1)
+        mm_blend(0, 2, False)
+        mm_blend(0, 3, False)
         turn("b", 1, 1, 0)
         blend(1, 1, 0)
-        mm_blend(0, 2, False)
         turn("b", 1, 1, 1)
         direct_mul("b", 1, 1)
         blend(1, 1, 1)
         blend(1, 1, 2)
         direct_add(1, 1)
         direct_gather(1)
-        back = turn_back(1, 0, 1, 0)
-        gather(back, 1, 0, 1, True)
-        back = turn_back(1, 1, 1, 1)
-        gather(back, 1, 1, 1, True)
-        mm_blend(0, 3, False)
-        back = turn_back(1, 2, 1, 2)
-        gather(back, 1, 2, 1, True)
+        for b in range(3):
+            back = turn_back(1, b, 1, b)
+            gather(back, 1, b, 1, True)
+        for r in range(4):
+            mm_given(1, r, False)
         for r in range(4):
             quantise_em(1, r, 1)
         for r in range(4):

@@ -17,6 +17,11 @@ ALU = mybir.AluOpType
 COPY = mybir.ActivationFunctionType.Copy
 
 P = 128
+TURNED = (0, 1, 2)
+BANK_A, BANK_B = 0, 2
+BANK_OUT = 4
+BANK_SPARE = 7
+SCALAR_COLUMNS = 128
 
 
 def tile_mix_blended_weights_and_given_pl_kernel(
@@ -28,80 +33,86 @@ def tile_mix_blended_weights_and_given_pl_kernel(
         psum = ctx.enter_context(tc.psum_pool(name="psum", bufs=1))
         ctx.enter_context(tc.manual_schedule())
 
-        def sb(name, shape, dtype):
+        def sbuf(name, shape, dtype):
             return keep.tile(shape, dtype, name=name, align_bytes=64)
 
-        def bank(i, name):
-            return psum.tile([P, 512], F32, name=name, tag="bank%d" % i)
+        def bank(index, name):
+            return psum.tile([P, 512], F32, name=name, tag="bank%d" % index)
 
-        ident = sb("ident", [P, P], F32)
-        sh_col = sb("sh_col", [P, 4], F32)
-        rest_col = sb("rest_col", [P, 4], F32)
-        warm_in = sb("warm_in", [P, 1], F32)
-        warm_out = sb("warm_out", [P, 1], F32)
-        ws_raw = sb("ws_raw", [P, 1024], U8)
-        xq_s = sb("xq_s", [P, 1024], U8)
-        xt_s = sb("xt_s", [P, 1024], U8)
-        wq_raw = sb("wq_raw", [P, 2048], U8)
-        wq_w = [sb("wq_w%d" % g, [P, 1024], U8) for g in range(2)]
-        wq_s = [sb("wq_s%d" % g, [P, 512], U8) for g in range(2)]
-        xq_w = [sb("xq_w%d" % g, [P, 2048], U8) for g in range(2)]
-        xt_w = [sb("xt_w%d" % g, [P, 1024], U8) for g in range(2)]
-        em_w = [sb("em_w%d" % g, [P, 512], U32) for g in range(2)]
-        em_s = [sb("em_s%d" % g, [P, 512], U8) for g in range(2)]
-        grouped = [sb("grouped%d" % g, [P, 2048], BF16) for g in range(2)]
+        ident = sbuf("ident", [P, P], F32)
+        sh_blocks = sbuf("sh_blocks", [P, P], F32)
+        sh_col = sbuf("sh_col", [P, 4], F32)
+        rest_col = sbuf("rest_col", [P, 4], F32)
+        sh_row = sbuf("sh_row", [P, P], F32)
+        rest_row = sbuf("rest_row", [P, P], F32)
+        wq_raw = sbuf("wq_raw", [P, 2048], U8)
+        wq_raw_s = sbuf("wq_raw_s", [P, 1024], U8)
+        wq_w = [sbuf("wq_w%d" % g, [P, 1024], U8) for g in range(2)]
+        wq_s = [sbuf("wq_s%d" % g, [P, 512], U8) for g in range(2)]
+        xq_w = [sbuf("xq_w%d" % g, [P, 2048], U8) for g in range(2)]
+        xq_s = sbuf("xq_s", [P, 1024], U8)
+        xt_w = [sbuf("xt_w%d" % g, [P, 1024], U8) for g in range(2)]
+        xt_s = sbuf("xt_s", [P, 1024], U8)
+        em_as_loaded = [sbuf("em_as_loaded%d" % g, [P, 512], BF16) for g in range(2)]
+        em_grouped = [sbuf("em_grouped%d" % g, [P, 2048], BF16) for g in range(2)]
+        em_w = [sbuf("em_w%d" % g, [P, 512], U32) for g in range(2)]
+        em_s = [sbuf("em_s%d" % g, [P, 512], U8) for g in range(2)]
+        zeros = sbuf("zeros", [P, 512], BF16)
+        zero_w = sbuf("zero_w", [P, P], U32)
+        zero_s = sbuf("zero_s", [P, P], U8)
+        table_in = sbuf("table_in", [P, 1], F32)
+        table_out = sbuf("table_out", [P, 1], F32)
 
-        zeros = sb("zeros", [P, 512], BF16)
-        zero_w = sb("zero_w", [P, 128], U32)
-        zero_s = sb("zero_s", [P, 128], U8)
-        sh_rows = sb("sh_rows", [P, 128], F32)
-        sh_row = sb("sh_row", [P, 128], F32)
-        rest_row = sb("rest_row", [P, 128], F32)
-        direct = [sb("direct%d" % g, [P, 512], BF16) for g in range(2)]
-
-        nc.gpsimd.memset(sh_rows[:], 0.0)
-        nc.gpsimd.memset(ws_raw[:].bitcast(I32), 0)
+        nc.gpsimd.memset(sh_blocks[:], 0.0)
+        nc.gpsimd.memset(wq_raw_s[:].bitcast(I32), 0)
         nc.vector.memset(zeros[:].bitcast(I32), 0)
-        nc.vector.memset(warm_in[:], 0.0)
+        nc.vector.memset(table_in[:], 0.0)
         nc.vector.quantize_mx(out=zero_w[:].bitcast(FP8X4), scales=zero_s[:], in_=zeros[:])
         nc.vector.memset(xq_s[:].bitcast(I32), 0)
         nc.vector.memset(xt_s[:].bitcast(I32), 0)
-        nc.scalar.dma_start(out=sh_rows[0:4, :], in_=sh.rearrange("o (b q) -> (o b) q", q=P))
-        nc.scalar.activation(out=warm_out[:], in_=warm_in[:], func=COPY)
+        nc.scalar.dma_start(out=sh_blocks[0:4, :], in_=sh.rearrange("o (b q) -> (o b) q", q=P))
+        nc.scalar.activation(out=table_out[:], in_=table_in[:], func=COPY)
         make_identity(nc, ident[:])
 
-        raw = {}
+        loaded = {}
 
-        def load_rows(which, src, g, u, h0, h1):
-            t = sb("raw_%s%d%d%d" % (which, g, u, h0), [P, 2, 256 * (h1 - h0)], F32)
-            rows = src[512 * g : 512 * (g + 1), :].rearrange("(p j) n -> p j n", j=4)
-            nc.sync.dma_start(out=t[:], in_=rows[:, 2 * u : 2 * u + 2, 256 * h0 : 256 * h1])
-            for h in range(h0, h1):
-                raw[which, g, u, h] = t[:, :, 256 * (h - h0) : 256 * (h - h0 + 1)]
+        def load_rows(matrix, g, u, halves=(0, 1)):
+            source = ea if matrix == "a" else eb
+            tile = sbuf("rows_%s%d%d%d" % (matrix, g, u, halves[0]), [P, 2, 256 * len(halves)], F32)
+            rows = source[512 * g : 512 * (g + 1), :].rearrange("(p j) n -> p j n", j=4)
+            nc.sync.dma_start(out=tile[:], in_=rows[:, 2 * u : 2 * u + 2, 256 * halves[0] : 256 * (halves[-1] + 1)])
+            for i, h in enumerate(halves):
+                loaded[matrix, g, u, h] = tile[:, :, 256 * i : 256 * (i + 1)]
 
-        def load_scales(queue, dst, src):
-            rows = src.bitcast(I32).rearrange("g (q r) c -> r q g c", r=4)
-            view = dst[:].bitcast(I32).rearrange("p (g c) -> p g c", g=2)
-            for r in range(4):
-                queue.dma_start(out=view[r:P:32], in_=rows[r])
+        def load_scales(planes, scales):
+            rows = scales.bitcast(I32).rearrange("g (q i) c -> i q g c", i=4)
+            view = planes[:].bitcast(I32).rearrange("p (g c) -> p g c", g=2)
+            for i in range(4):
+                nc.sync.dma_start(out=view[i:P:32], in_=rows[i])
 
-        load_rows("a", ea, 0, 0, 0, 2)
-        load_scales(nc.sync, ws_raw, wq_scales)
+        def load_xq(g):
+            nc.sync.dma_start(out=xq_w[g][:], in_=xq_words[g].rearrange("p c j -> p (c j)"))
+
+        def load_xt(g):
+            nc.sync.dma_start(out=xt_w[g][:], in_=xt_words[g])
+
         nc.sync.dma_start(out=wq_raw[:].rearrange("p (g c) -> p g c", g=2), in_=wq_words.rearrange("g p c -> p g c"))
-        load_rows("b", eb, 0, 0, 0, 2)
-        nc.sync.dma_start(out=xq_w[0][:], in_=xq_words[0].rearrange("p c r -> p (c r)"))
-        load_scales(nc.sync, xq_s, xq_scales)
-        load_rows("a", ea, 0, 1, 0, 2)
-        load_rows("b", eb, 0, 1, 0, 2)
-        load_rows("a", ea, 1, 0, 0, 2)
-        load_rows("b", eb, 1, 0, 0, 2)
-        load_scales(nc.sync, xt_s, xt_scales)
-        nc.sync.dma_start(out=xt_w[0][:], in_=xt_words[0])
-        load_rows("a", ea, 1, 1, 0, 2)
-        load_rows("b", eb, 1, 1, 0, 1)
-        load_rows("b", eb, 1, 1, 1, 2)
-        nc.sync.dma_start(out=xq_w[1][:], in_=xq_words[1].rearrange("p c r -> p (c r)"))
-        nc.sync.dma_start(out=xt_w[1][:], in_=xt_words[1])
+        load_scales(wq_raw_s, wq_scales)
+        load_rows("a", 0, 0)
+        load_rows("b", 0, 0)
+        load_xq(0)
+        load_scales(xq_s, xq_scales)
+        load_rows("a", 0, 1)
+        load_rows("b", 0, 1)
+        load_xq(1)
+        load_rows("a", 1, 0)
+        load_rows("b", 1, 0)
+        load_scales(xt_s, xt_scales)
+        load_xt(0)
+        load_rows("a", 1, 1)
+        load_rows("b", 1, 1, (0,))
+        load_rows("b", 1, 1, (1,))
+        load_xt(1)
 
         def deal_words(g):
             nc.vector.tensor_copy(
@@ -112,68 +123,115 @@ def tile_mix_blended_weights_and_given_pl_kernel(
         def deal_scales(g):
             nc.vector.tensor_copy(
                 out=wq_s[g][:].rearrange("p (r m) -> p r m", r=4),
-                in_=ws_raw[:, 512 * g : 512 * (g + 1)].rearrange("p (m r) -> p r m", r=4),
+                in_=wq_raw_s[:, 512 * g : 512 * (g + 1)].rearrange("p (m r) -> p r m", r=4),
             )
 
-        acc = [bank(4 + r, "acc%d" % r) for r in range(4)]
         turned = {}
-        part = {}
-        emt = {}
+        a_part = {}
+        em_turned = {}
+        product = {}
+        acc = {}
 
-        def turn(which, g, u, h):
-            t = bank(h if which == "a" else 2 + h, "turned_%s%d%d%d" % (which, g, u, h))
-            turned[which, g, u, h] = t
-            for bb in range(2 - h):
-                for e in range(2):
-                    c = 128 * (2 * bb + e)
-                    nc.tensor.transpose(t[:, c : c + 128], raw[which, g, u, h][:, e, 128 * bb : 128 * (bb + 1)], ident[:])
+        def turn(matrix, g, u, halves=(0, 1)):
+            for h in halves:
+                tile = bank((BANK_A if matrix == "a" else BANK_B) + h, "turned_%s%d%d%d" % (matrix, g, u, h))
+                for i, b in enumerate(b for b in TURNED if b // 2 == h):
+                    for e in range(2):
+                        c = 256 * i + P * e
+                        nc.tensor.transpose(tile[:, c : c + P], loaded[matrix, g, u, h][:, e, P * i : P * (i + 1)], ident[:])
+                    turned[matrix, g, u, b] = tile[:, 256 * i : 256 * (i + 1)].rearrange("q (e p) -> q p e", e=2)
 
-        def pairs(t, bb):
-            return t[:, 256 * bb : 256 * (bb + 1)].rearrange("q (e p) -> q p e", e=2)
+        def scale_a(g, u, blocks=TURNED):
+            for b in blocks:
+                tile = sbuf("a_part%d%d%d" % (g, u, b), [P, 256], F32)
+                a_part[g, u, b] = tile[:].rearrange("q (p e) -> q p e", e=2)
+                nc.scalar.activation(out=a_part[g, u, b], in_=turned["a", g, u, b], func=COPY, scale=sh_col[:, b : b + 1])
 
-        def scale_a(g, u, b):
-            t = sb("part%d%d%d" % (g, u, b), [P, 256], F32)
-            part[g, u, b] = t
-            nc.scalar.activation(
-                out=t[:].rearrange("q (p e) -> q p e", e=2),
-                in_=pairs(turned["a", g, u, b // 2], b % 2),
-                func=COPY,
-                scale=sh_col[:, b : b + 1],
+        def blend(g, u, blocks=TURNED):
+            for b in blocks:
+                tile = sbuf("em_turned%d%d%d" % (g, u, b), [P, 256], BF16)
+                em_turned[g, u, b] = tile
+                nc.vector.scalar_tensor_tensor(
+                    out=tile[:].rearrange("q (p e) -> q p e", e=2),
+                    in0=turned["b", g, u, b],
+                    scalar=rest_col[:, b : b + 1],
+                    in1=a_part[g, u, b],
+                    op0=ALU.mult,
+                    op1=ALU.add,
+                )
+
+        def turn_back_and_group(g, first, count, index):
+            tile = bank(index, "back%d%d" % (g, first))
+            for i in range(count):
+                for u in range(2):
+                    c = P * (u * count + i)
+                    nc.tensor.transpose(tile[:, c : c + P], em_turned[g, u, first + i][:].bitcast(F32), ident[:])
+            words = em_grouped[g][:].bitcast(F32).rearrange("p (r m u) -> p r m u", r=4, u=2)
+            nc.scalar.copy(
+                out=words[:, :, 32 * first : 32 * (first + count), :],
+                in_=tile[:, 0 : 256 * count].rearrange("p (u m r) -> p r m u", u=2, r=4),
             )
 
-        prod = {}
-
-        def direct_mul(which, g, u):
-            t = sb("prod_%s%d%d" % (which, g, u), [P, 2, 128], F32)
-            prod[which, g, u] = t
-            row = sh_row if which == "a" else rest_row
-            engine = nc.vector if (which, g, u) == ("a", 0, 0) else nc.gpsimd
-            engine.tensor_tensor(
-                out=t[:],
-                in0=raw[which, g, u, 1][:, :, 128:256],
-                in1=row[:].unsqueeze(1).broadcast_to([P, 2, 128]),
+        def multiply_as_loaded(matrix, g, u):
+            tile = sbuf("product_%s%d%d" % (matrix, g, u), [P, 2, P], F32)
+            product[matrix, g, u] = tile[:].rearrange("p e n -> p (e n)")
+            share = sh_row if matrix == "a" else rest_row
+            nc.vector.tensor_tensor(
+                out=tile[:],
+                in0=loaded[matrix, g, u, 1][:, :, P : 2 * P],
+                in1=share[:].unsqueeze(1).broadcast_to([P, 2, P]),
                 op=ALU.mult,
             )
 
-        def direct_add(g, u):
-            engine = nc.vector if (g, u) == (1, 1) else nc.gpsimd
-            engine.tensor_tensor(
-                out=direct[g][:, 256 * u : 256 * (u + 1)],
-                in0=prod["a", g, u][:].rearrange("p e n -> p (e n)"),
-                in1=prod["b", g, u][:].rearrange("p e n -> p (e n)"),
-                op=ALU.add,
+        def add_as_loaded(g, u):
+            nc.vector.tensor_tensor(
+                out=em_as_loaded[g][:, 256 * u : 256 * (u + 1)], in0=product["a", g, u], in1=product["b", g, u], op=ALU.add
             )
 
-        def direct_gather(g):
+        def group_as_loaded(g):
             nc.vector.tensor_copy(
-                out=grouped[g][:].rearrange("p (r m j) -> p r m j", r=4, j=4)[:, :, 96:128, :],
-                in_=direct[g][:].rearrange("p (j m r) -> p r m j", j=4, r=4),
+                out=em_grouped[g][:].rearrange("p (r m j) -> p r m j", r=4, j=4)[:, :, 96:128, :],
+                in_=em_as_loaded[g][:].rearrange("p (j m r) -> p r m j", j=4, r=4),
             )
 
-        def warm(count):
-            for i in range(count):
+        def quantise_em(g, first, count):
+            nc.vector.quantize_mx(
+                out=em_w[g][:, P * first : P * (first + count)].bitcast(FP8X4),
+                scales=em_s[g][:, P * first : P * (first + count)],
+                in_=em_grouped[g][:, 512 * first : 512 * (first + count)],
+            )
+
+        def given_pass(g, tiles):
+            for r in tiles:
+                if g == 0:
+                    acc[r] = bank(BANK_OUT + r, "acc%d" % r)
                 nc.tensor.matmul_mx(
-                    out=acc[3][:, 0:128],
+                    out=acc[r][:],
+                    lhsT=wq_w[g][:, 256 * r : 256 * (r + 1)].bitcast(FP4X4),
+                    lhsT_scale=wq_s[g][:, P * r : P * (r + 1)],
+                    rhs=xq_w[g][:].bitcast(FP8X4),
+                    rhs_scale=xq_s[:, 512 * g : 512 * (g + 1)],
+                    start=(g == 0),
+                    stop=False,
+                )
+
+        def blended_pass(g, tiles):
+            for r in tiles:
+                nc.tensor.matmul_mx(
+                    out=acc[r][:],
+                    lhsT=em_w[g][:, P * r : P * (r + 1)].bitcast(FP8X4),
+                    lhsT_scale=em_s[g][:, P * r : P * (r + 1)],
+                    rhs=xt_w[g][:].bitcast(FP4X4),
+                    rhs_scale=xt_s[:, 512 * g : 512 * (g + 1)],
+                    start=False,
+                    stop=(g == 1),
+                )
+
+        def warm_up(name, count):
+            idle = bank(BANK_SPARE, name)
+            for repeat in range(count):
+                nc.tensor.matmul_mx(
+                    out=idle[:, 0:P],
                     lhsT=zero_w[:].bitcast(FP8X4),
                     lhsT_scale=zero_s[:],
                     rhs=zero_w[:].bitcast(U8)[:, 0:256].bitcast(FP4X4),
@@ -182,166 +240,107 @@ def tile_mix_blended_weights_and_given_pl_kernel(
                     stop=True,
                 )
 
-        def blend(g, u, b):
-            t = sb("emt%d%d%d" % (g, u, b), [P, 256], BF16)
-            emt[g, u, b] = t
-            nc.vector.scalar_tensor_tensor(
-                out=t[:].rearrange("q (p e) -> q p e", e=2),
-                in0=pairs(turned["b", g, u, b // 2], b % 2),
-                scalar=rest_col[:, b : b + 1],
-                in1=part[g, u, b][:].rearrange("q (p e) -> q p e", e=2),
-                op0=ALU.mult,
-                op1=ALU.add,
-            )
+        warm_up("idle_before_sh", 10)
+        columns = bank(BANK_B, "columns")
+        nc.tensor.transpose(columns[:, 0:P], sh_blocks[:], ident[:])
+        nc.scalar.copy(out=sh_col[:], in_=columns[:, 0:4])
+        nc.scalar.activation(out=rest_col[:], in_=columns[:, 0:4], func=COPY, scale=-1.0, bias=1.0)
+        warm_up("idle_before_spread", 3)
+        spread = bank(BANK_B + 1, "spread")
+        nc.tensor.transpose(spread[:, 0:P], sh_col[:, 3:4].to_broadcast([P, P]), ident[:])
+        nc.scalar.copy(out=sh_row[:], in_=spread[:, 0:P])
+        nc.scalar.activation(out=rest_row[:], in_=spread[:, 0:P], func=COPY, scale=-1.0, bias=1.0)
+        warm_up("idle_before_ea", 3)
 
-        def turn_back(g, b0, nb, i):
-            t = bank(i, "back%d%d" % (g, b0))
-            for bb in range(nb):
-                for u in range(2):
-                    c = 128 * (u * nb + bb)
-                    nc.tensor.transpose(t[:, c : c + 128], emt[g, u, b0 + bb][:].bitcast(F32), ident[:])
-            return t
-
-        def gather(t, g, b0, nb, on_scalar):
-            src = t[:, 0 : 256 * nb].rearrange("p (u m r) -> p r m u", u=2, r=4)
-            dst = grouped[g][:].bitcast(F32).rearrange("p (r m u) -> p r m u", r=4, u=2)[:, :, 32 * b0 : 32 * (b0 + nb), :]
-            if on_scalar:
-                nc.scalar.copy(out=dst, in_=src)
-            else:
-                nc.vector.tensor_copy(out=dst, in_=src)
-
-        def quantise_em(g, r0, nr):
-            nc.vector.quantize_mx(
-                out=em_w[g][:, 128 * r0 : 128 * (r0 + nr)].bitcast(FP8X4),
-                scales=em_s[g][:, 128 * r0 : 128 * (r0 + nr)],
-                in_=grouped[g][:, 512 * r0 : 512 * (r0 + nr)],
-            )
-
-        def mm_given(g, r, start):
-            nc.tensor.matmul_mx(
-                out=acc[r][:],
-                lhsT=wq_w[g][:, 256 * r : 256 * (r + 1)].bitcast(FP4X4),
-                lhsT_scale=wq_s[g][:, 128 * r : 128 * (r + 1)],
-                rhs=xq_w[g][:].bitcast(FP8X4),
-                rhs_scale=xq_s[:, 512 * g : 512 * (g + 1)],
-                start=start,
-                stop=False,
-            )
-
-        def mm_blend(g, r, stop):
-            nc.tensor.matmul_mx(
-                out=acc[r][:],
-                lhsT=em_w[g][:, 128 * r : 128 * (r + 1)].bitcast(FP8X4),
-                lhsT_scale=em_s[g][:, 128 * r : 128 * (r + 1)],
-                rhs=xt_w[g][:].bitcast(FP4X4),
-                rhs_scale=xt_s[:, 512 * g : 512 * (g + 1)],
-                start=False,
-                stop=stop,
-            )
-
-        def turn_both(which, g, u):
-            for h in range(2):
-                turn(which, g, u, h)
-
-        def a_side(g, u):
-            turn_both("a", g, u)
-            for b in range(3):
-                scale_a(g, u, b)
-            direct_mul("a", g, u)
-
-        def b_side(g, u):
-            turn_both("b", g, u)
-            direct_mul("b", g, u)
-            for b in range(3):
-                blend(g, u, b)
-            direct_add(g, u)
-
-        warm(12)
-        columns = bank(2, "columns")
-        nc.tensor.transpose(columns[:, 0:128], sh_rows[:], ident[:])
-        nc.vector.tensor_copy(out=sh_col[:], in_=columns[:, 0:4])
-        nc.vector.tensor_scalar(out=rest_col[:], in0=columns[:, 0:4], scalar1=-1.0, scalar2=1.0, op0=ALU.mult, op1=ALU.add)
-        warm(3)
-        spread = bank(3, "spread")
-        nc.tensor.transpose(spread[:, 0:128], sh_col[:, 3:4].to_broadcast([P, P]), ident[:])
-        nc.vector.tensor_copy(out=sh_row[:], in_=spread[:, 0:128])
-        nc.vector.tensor_scalar(out=rest_row[:], in0=spread[:, 0:128], scalar1=-1.0, scalar2=1.0, op0=ALU.mult, op1=ALU.add)
-        a_side(0, 0)
-        warm(8)
         deal_words(0)
         deal_scales(0)
+        turn("a", 0, 0)
+        scale_a(0, 0)
+        warm_up("idle_before_eb", 6)
+        multiply_as_loaded("a", 0, 0)
         deal_words(1)
+        turn("b", 0, 0)
+        multiply_as_loaded("b", 0, 0)
+        blend(0, 0)
+        add_as_loaded(0, 0)
         deal_scales(1)
-        b_side(0, 0)
-        mm_given(0, 0, True)
-        mm_given(0, 1, True)
-        a_side(0, 1)
-        mm_given(0, 2, True)
-        b_side(0, 1)
-        mm_given(0, 3, True)
-        back = turn_back(0, 0, 2, 2)
-        gather(back, 0, 0, 2, True)
-        turn_both("a", 1, 0)
-        back = turn_back(0, 2, 1, 3)
-        gather(back, 0, 2, 1, True)
-        direct_gather(0)
+        given_pass(0, (0, 1))
+
+        turn("a", 0, 1)
+        scale_a(0, 1)
+        multiply_as_loaded("a", 0, 1)
+        given_pass(0, (2,))
+        turn("b", 0, 1)
+        multiply_as_loaded("b", 0, 1)
+        blend(0, 1)
+        add_as_loaded(0, 1)
+        given_pass(1, (0, 1))
+
+        turn_back_and_group(0, 0, 2, BANK_B)
+        turn("a", 1, 0)
+        scale_a(1, 0, (0,))
+        turn_back_and_group(0, 2, 1, BANK_SPARE)
+        scale_a(1, 0, (1, 2))
+        group_as_loaded(0)
+        multiply_as_loaded("a", 1, 0)
+        given_pass(1, (2,))
+        turn("b", 1, 0)
+        multiply_as_loaded("b", 1, 0)
         quantise_em(0, 0, 4)
-        for b in range(3):
-            scale_a(1, 0, b)
-        direct_mul("a", 1, 0)
-        b_side(1, 0)
-        mm_blend(0, 0, False)
-        mm_blend(0, 1, False)
-        a_side(1, 1)
-        mm_blend(0, 2, False)
-        mm_blend(0, 3, False)
-        turn("b", 1, 1, 0)
-        blend(1, 1, 0)
-        turn("b", 1, 1, 1)
-        direct_mul("b", 1, 1)
-        blend(1, 1, 1)
-        blend(1, 1, 2)
-        direct_add(1, 1)
-        direct_gather(1)
-        for b in range(3):
-            back = turn_back(1, b, 1, b)
-            gather(back, 1, b, 1, True)
-        for r in range(4):
-            mm_given(1, r, False)
+        blend(1, 0)
+        add_as_loaded(1, 0)
+        given_pass(0, (3,))
+        given_pass(1, (3,))
+
+        turn("a", 1, 1)
+        scale_a(1, 1)
+        multiply_as_loaded("a", 1, 1)
+        turn("b", 1, 1, (0,))
+        blend(1, 1, (0, 1))
+        blended_pass(0, (0,))
+        turn("b", 1, 1, (1,))
+        multiply_as_loaded("b", 1, 1)
+        blend(1, 1, (2,))
+        add_as_loaded(1, 1)
+        group_as_loaded(1)
+        turn_back_and_group(1, 0, 1, BANK_A)
+        turn_back_and_group(1, 1, 1, BANK_A + 1)
+        blended_pass(0, (1,))
+        turn_back_and_group(1, 2, 1, BANK_B)
+        blended_pass(0, (2, 3))
         for r in range(4):
             quantise_em(1, r, 1)
-        for r in range(4):
-            mm_blend(1, r, True)
+        blended_pass(1, range(4))
 
-        y = sb("y", [P, 4, T], F32)
-        y_bf = [sb("y_bf%d" % h, [P, 1024], BF16) for h in range(2)]
-        y_w = sb("y_w", [P, T], U32)
-        y_s = sb("y_s", [P, T], U8)
+        y = sbuf("y", [P, 4, T], F32)
+        y_grouped = [sbuf("y_grouped%d" % h, [P, 1024], BF16) for h in range(2)]
+        y_w = sbuf("y_w", [P, T], U32)
+        y_s = sbuf("y_s", [P, T], U8)
         out_rows = out_0.rearrange("(p r) t -> p r t", r=4)
         nc.vector.tensor_copy(out=y[:, 0, :], in_=acc[0][:])
+        nc.sync.dma_start(out=out_rows[:, 0, :], in_=y[:, 0, :])
         nc.scalar.copy(out=y[:, 1, :], in_=acc[1][:])
-        nc.sync.dma_start(out=out_rows[:, 0:2, :], in_=y[:, 0:2, :])
+        nc.sync.dma_start(out=out_rows[:, 1, :], in_=y[:, 1, :])
         nc.vector.tensor_copy(out=y[:, 2, :], in_=acc[2][:])
+        nc.sync.dma_start(out=out_rows[:, 2, :], in_=y[:, 2, :])
         nc.scalar.copy(out=y[:, 3, 0:256], in_=acc[3][:, 0:256])
         nc.scalar.copy(out=y[:, 3, 256:512], in_=acc[3][:, 256:512])
-        nc.sync.dma_start(out=out_rows[:, 2:4, :], in_=y[:, 2:4, :])
+        nc.sync.dma_start(out=out_rows[:, 3, :], in_=y[:, 3, :])
 
-        def weave(h, c0, c1, on_scalar):
-            dst = y_bf[h][:, 4 * c0 : 4 * c1].rearrange("p (c i r) -> p c r i", i=4, r=4)
-            src = y[:, :, 256 * h + c0 : 256 * h + c1].rearrange("p r (c i) -> p c r i", i=4)
-            if on_scalar:
-                nc.scalar.copy(out=dst, in_=src)
-            else:
-                nc.vector.tensor_copy(out=dst, in_=src)
+        def group_result(copy, h, first, last):
+            copy(
+                out=y_grouped[h][:, 4 * first : 4 * last].rearrange("p (c i r) -> p c r i", i=4, r=4),
+                in_=y[:, :, 256 * h + first : 256 * h + last].rearrange("p r (c i) -> p c r i", i=4),
+            )
 
-        weave(0, 0, 256, False)
-        weave(1, 0, 128, True)
-        weave(1, 128, 256, False)
-        words_out = out_1[0].rearrange("p c r -> p (c r)").bitcast(I32)
+        group_result(nc.vector.tensor_copy, 0, 0, 256)
+        group_result(nc.scalar.copy, 1, 0, SCALAR_COLUMNS)
+        group_result(nc.vector.tensor_copy, 1, SCALAR_COLUMNS, 256)
+        words_out = out_1[0].rearrange("p c j -> p (c j)").bitcast(I32)
         for h in range(2):
-            cols = slice(256 * h, 256 * (h + 1))
-            nc.vector.quantize_mx(out=y_w[:, cols].bitcast(FP8X4), scales=y_s[:, cols], in_=y_bf[h][:])
-            nc.sync.dma_start(out=words_out[:, cols], in_=y_w[:, cols].bitcast(I32))
+            tokens = slice(256 * h, 256 * (h + 1))
+            nc.vector.quantize_mx(out=y_w[:, tokens].bitcast(FP8X4), scales=y_s[:, tokens], in_=y_grouped[h][:])
+            nc.sync.dma_start(out=words_out[:, tokens], in_=y_w[:, tokens].bitcast(I32))
         for q in range(4):
             queue = nc.sync if q % 2 == 0 else nc.scalar
             queue.dma_start(out=out_2[0].bitcast(I32)[4 * q : 4 * q + 4, :], in_=y_s[:].bitcast(I32)[32 * q : 32 * q + 4, :])

@@ -57,21 +57,12 @@ def tile_mix_blended_weights_and_given_pl_kernel(
         em_grouped = [sbuf("em_grouped%d" % g, [P, 2048], BF16) for g in range(2)]
         em_w = [sbuf("em_w%d" % g, [P, 512], U32) for g in range(2)]
         em_s = [sbuf("em_s%d" % g, [P, 512], U8) for g in range(2)]
-        zeros = sbuf("zeros", [P, 512], BF16)
-        zero_w = sbuf("zero_w", [P, P], U32)
-        zero_s = sbuf("zero_s", [P, P], U8)
-        table_in = sbuf("table_in", [P, 1], F32)
-        table_out = sbuf("table_out", [P, 1], F32)
 
         nc.gpsimd.memset(sh_blocks[:], 0.0)
         nc.gpsimd.memset(wq_raw_s[:].bitcast(I32), 0)
-        nc.vector.memset(zeros[:].bitcast(I32), 0)
-        nc.vector.memset(table_in[:], 0.0)
-        nc.vector.quantize_mx(out=zero_w[:].bitcast(FP8X4), scales=zero_s[:], in_=zeros[:])
         nc.vector.memset(xq_s[:].bitcast(I32), 0)
         nc.vector.memset(xt_s[:].bitcast(I32), 0)
         nc.scalar.dma_start(out=sh_blocks[0:4, :], in_=sh.rearrange("o (b q) -> (o b) q", q=P))
-        nc.scalar.activation(out=table_out[:], in_=table_in[:], func=COPY)
         make_identity(nc, ident[:])
 
         loaded = {}
@@ -84,11 +75,11 @@ def tile_mix_blended_weights_and_given_pl_kernel(
             for i, h in enumerate(halves):
                 loaded[matrix, g, u, h] = tile[:, :, 256 * i : 256 * (i + 1)]
 
-        def load_scales(planes, scales):
+        def load_scales(queue, planes, scales):
             rows = scales.bitcast(I32).rearrange("g (q i) c -> i q g c", i=4)
             view = planes[:].bitcast(I32).rearrange("p (g c) -> p g c", g=2)
             for i in range(4):
-                nc.sync.dma_start(out=view[i:P:32], in_=rows[i])
+                queue.dma_start(out=view[i:P:32], in_=rows[i])
 
         def load_xq(g):
             nc.sync.dma_start(out=xq_w[g][:], in_=xq_words[g].rearrange("p c j -> p (c j)"))
@@ -96,22 +87,22 @@ def tile_mix_blended_weights_and_given_pl_kernel(
         def load_xt(g):
             nc.sync.dma_start(out=xt_w[g][:], in_=xt_words[g])
 
+        load_scales(nc.gpsimd, xt_s, xt_scales)
         nc.sync.dma_start(out=wq_raw[:].rearrange("p (g c) -> p g c", g=2), in_=wq_words.rearrange("g p c -> p g c"))
-        load_scales(wq_raw_s, wq_scales)
+        load_scales(nc.sync, wq_raw_s, wq_scales)
         load_rows("a", 0, 0)
         load_rows("b", 0, 0)
         load_xq(0)
-        load_scales(xq_s, xq_scales)
+        load_scales(nc.sync, xq_s, xq_scales)
         load_rows("a", 0, 1)
         load_rows("b", 0, 1)
         load_xq(1)
         load_rows("a", 1, 0)
         load_rows("b", 1, 0)
-        load_scales(xt_s, xt_scales)
-        load_xt(0)
         load_rows("a", 1, 1)
         load_rows("b", 1, 1, (0,))
         load_rows("b", 1, 1, (1,))
+        load_xt(0)
         load_xt(1)
 
         def deal_words(g):
@@ -227,36 +218,19 @@ def tile_mix_blended_weights_and_given_pl_kernel(
                     stop=(g == 1),
                 )
 
-        def warm_up(name, count):
-            idle = bank(BANK_SPARE, name)
-            for repeat in range(count):
-                nc.tensor.matmul_mx(
-                    out=idle[:, 0:P],
-                    lhsT=zero_w[:].bitcast(FP8X4),
-                    lhsT_scale=zero_s[:],
-                    rhs=zero_w[:].bitcast(U8)[:, 0:256].bitcast(FP4X4),
-                    rhs_scale=zero_s[:],
-                    start=True,
-                    stop=True,
-                )
-
-        warm_up("idle_before_sh", 10)
         columns = bank(BANK_B, "columns")
         nc.tensor.transpose(columns[:, 0:P], sh_blocks[:], ident[:])
-        nc.scalar.copy(out=sh_col[:], in_=columns[:, 0:4])
         nc.scalar.activation(out=rest_col[:], in_=columns[:, 0:4], func=COPY, scale=-1.0, bias=1.0)
-        warm_up("idle_before_spread", 3)
+        nc.scalar.copy(out=sh_col[:], in_=columns[:, 0:4])
         spread = bank(BANK_B + 1, "spread")
         nc.tensor.transpose(spread[:, 0:P], sh_col[:, 3:4].to_broadcast([P, P]), ident[:])
         nc.scalar.copy(out=sh_row[:], in_=spread[:, 0:P])
         nc.scalar.activation(out=rest_row[:], in_=spread[:, 0:P], func=COPY, scale=-1.0, bias=1.0)
-        warm_up("idle_before_ea", 3)
 
         deal_words(0)
         deal_scales(0)
         turn("a", 0, 0)
         scale_a(0, 0)
-        warm_up("idle_before_eb", 6)
         multiply_as_loaded("a", 0, 0)
         deal_words(1)
         turn("b", 0, 0)
@@ -297,7 +271,6 @@ def tile_mix_blended_weights_and_given_pl_kernel(
         multiply_as_loaded("a", 1, 1)
         turn("b", 1, 1, (0,))
         blend(1, 1, (0, 1))
-        blended_pass(0, (0,))
         turn("b", 1, 1, (1,))
         multiply_as_loaded("b", 1, 1)
         blend(1, 1, (2,))
@@ -305,20 +278,23 @@ def tile_mix_blended_weights_and_given_pl_kernel(
         group_as_loaded(1)
         turn_back_and_group(1, 0, 1, BANK_A)
         turn_back_and_group(1, 1, 1, BANK_A + 1)
-        blended_pass(0, (1,))
+        blended_pass(0, (0,))
         turn_back_and_group(1, 2, 1, BANK_B)
-        blended_pass(0, (2, 3))
+        blended_pass(0, (1, 2))
         for r in range(4):
             quantise_em(1, r, 1)
-        blended_pass(1, range(4))
+        blended_pass(1, (0, 1, 2))
+        blended_pass(0, (3,))
+        blended_pass(1, (3,))
 
         y = sbuf("y", [P, 4, T], F32)
         y_grouped = [sbuf("y_grouped%d" % h, [P, 1024], BF16) for h in range(2)]
         y_w = sbuf("y_w", [P, T], U32)
         y_s = sbuf("y_s", [P, T], U8)
         out_rows = out_0.rearrange("(p r) t -> p r t", r=4)
-        nc.vector.tensor_copy(out=y[:, 0, :], in_=acc[0][:])
-        nc.sync.dma_start(out=out_rows[:, 0, :], in_=y[:, 0, :])
+        for c in (0, 256):
+            nc.vector.tensor_copy(out=y[:, 0, c : c + 256], in_=acc[0][:, c : c + 256])
+            nc.sync.dma_start(out=out_rows[:, 0, c : c + 256], in_=y[:, 0, c : c + 256])
         nc.scalar.copy(out=y[:, 1, :], in_=acc[1][:])
         nc.sync.dma_start(out=out_rows[:, 1, :], in_=y[:, 1, :])
         nc.vector.tensor_copy(out=y[:, 2, :], in_=acc[2][:])
@@ -342,5 +318,4 @@ def tile_mix_blended_weights_and_given_pl_kernel(
             nc.vector.quantize_mx(out=y_w[:, tokens].bitcast(FP8X4), scales=y_s[:, tokens], in_=y_grouped[h][:])
             nc.sync.dma_start(out=words_out[:, tokens], in_=y_w[:, tokens].bitcast(I32))
         for q in range(4):
-            queue = nc.sync if q % 2 == 0 else nc.scalar
-            queue.dma_start(out=out_2[0].bitcast(I32)[4 * q : 4 * q + 4, :], in_=y_s[:].bitcast(I32)[32 * q : 32 * q + 4, :])
+            nc.scalar.dma_start(out=out_2[0].bitcast(I32)[4 * q : 4 * q + 4, :], in_=y_s[:].bitcast(I32)[32 * q : 32 * q + 4, :])

from contextlib import ExitStack

import concourse.mybir as mybir
from concourse.masks import make_identity

K, L, T, N = 1024, 1024, 512, 512
FLOPS = 2 * (K + L) * T * N

F32 = mybir.dt.float32
BF16 = mybir.dt.bfloat16
I32 = mybir.dt.int32
U32 = mybir.dt.uint32
U8 = mybir.dt.uint8
FP8X4 = mybir.dt.float8_e4m3fn_x4
FP4X4 = mybir.dt.float4_e2m1fn_x4
ALU = mybir.AluOpType
COPY = mybir.ActivationFunctionType.Copy

P = 128
TURNED = (0, 1, 2)
BANK_A, BANK_B = 0, 2
BANK_OUT = 4
BANK_SPARE = 7
SCALAR_COLUMNS = 128


def tile_mix_blended_weights_and_given_pl_kernel(
    tc, xt_words, xt_scales, ea, eb, sh, xq_words, xq_scales, wq_words, wq_scales, out_0, out_1, out_2
):
    nc = tc.nc
    with ExitStack() as ctx:
        keep = ctx.enter_context(tc.tile_pool(name="keep", bufs=1))
        psum = ctx.enter_context(tc.psum_pool(name="psum", bufs=1))
        ctx.enter_context(tc.manual_schedule())

        def sbuf(name, shape, dtype):
            return keep.tile(shape, dtype, name=name, align_bytes=64)

        def bank(index, name):
            return psum.tile([P, 512], F32, name=name, tag="bank%d" % index)

        ident = sbuf("ident", [P, P], F32)
        sh_blocks = sbuf("sh_blocks", [P, P], F32)
        sh_col = sbuf("sh_col", [P, 4], F32)
        rest_col = sbuf("rest_col", [P, 4], F32)
        sh_row = sbuf("sh_row", [P, P], F32)
        rest_row = sbuf("rest_row", [P, P], F32)
        wq_raw = sbuf("wq_raw", [P, 2048], U8)
        wq_raw_s = sbuf("wq_raw_s", [P, 1024], U8)
        wq_w = [sbuf("wq_w%d" % g, [P, 1024], U8) for g in range(2)]
        wq_s = [sbuf("wq_s%d" % g, [P, 512], U8) for g in range(2)]
        xq_w = [sbuf("xq_w%d" % g, [P, 2048], U8) for g in range(2)]
        xq_s = sbuf("xq_s", [P, 1024], U8)
        xt_w = [sbuf("xt_w%d" % g, [P, 1024], U8) for g in range(2)]
        xt_s = sbuf("xt_s", [P, 1024], U8)
        em_as_loaded = [sbuf("em_as_loaded%d" % g, [P, 512], BF16) for g in range(2)]
        em_grouped = [sbuf("em_grouped%d" % g, [P, 2048], BF16) for g in range(2)]
        em_w = [sbuf("em_w%d" % g, [P, 512], U32) for g in range(2)]
        em_s = [sbuf("em_s%d" % g, [P, 512], U8) for g in range(2)]

        nc.gpsimd.memset(sh_blocks[:], 0.0)
        nc.gpsimd.memset(wq_raw_s[:].bitcast(I32), 0)
        nc.vector.memset(xq_s[:].bitcast(I32), 0)
        nc.vector.memset(xt_s[:].bitcast(I32), 0)
        nc.scalar.dma_start(out=sh_blocks[0:4, :], in_=sh.rearrange("o (b q) -> (o b) q", q=P))
        make_identity(nc, ident[:])

        loaded = {}

        def load_rows(matrix, g, u, halves=(0, 1)):
            source = ea if matrix == "a" else eb
            tile = sbuf("rows_%s%d%d%d" % (matrix, g, u, halves[0]), [P, 2, 256 * len(halves)], F32)
            rows = source[512 * g : 512 * (g + 1), :].rearrange("(p j) n -> p j n", j=4)
            nc.sync.dma_start(out=tile[:], in_=rows[:, 2 * u : 2 * u + 2, 256 * halves[0] : 256 * (halves[-1] + 1)])
            for i, h in enumerate(halves):
                loaded[matrix, g, u, h] = tile[:, :, 256 * i : 256 * (i + 1)]

        def load_scales(queue, planes, scales):
            rows = scales.bitcast(I32).rearrange("g (q i) c -> i q g c", i=4)
            view = planes[:].bitcast(I32).rearrange("p (g c) -> p g c", g=2)
            for i in range(4):
                queue.dma_start(out=view[i:P:32], in_=rows[i])

        def load_xq(g):
            nc.sync.dma_start(out=xq_w[g][:], in_=xq_words[g].rearrange("p c j -> p (c j)"))

        def load_xt(g):
            nc.sync.dma_start(out=xt_w[g][:], in_=xt_words[g])

        load_scales(nc.gpsimd, xt_s, xt_scales)
        nc.sync.dma_start(out=wq_raw[:].rearrange("p (g c) -> p g c", g=2), in_=wq_words.rearrange("g p c -> p g c"))
        load_scales(nc.sync, wq_raw_s, wq_scales)
        load_rows("a", 0, 0)
        load_rows("b", 0, 0)
        load_xq(0)
        load_scales(nc.sync, xq_s, xq_scales)
        load_rows("a", 0, 1)
        load_rows("b", 0, 1)
        load_xq(1)
        load_rows("a", 1, 0)
        load_rows("b", 1, 0)
        load_rows("a", 1, 1)
        load_rows("b", 1, 1, (0,))
        load_rows("b", 1, 1, (1,))
        load_xt(0)
        load_xt(1)

        def deal_words(g):
            nc.vector.tensor_copy(
                out=wq_w[g][:].rearrange("p (r m z) -> p r m z", r=4, z=2),
                in_=wq_raw[:, 1024 * g : 1024 * (g + 1)].rearrange("p (m r z) -> p r m z", r=4, z=2),
            )

        def deal_scales(g):
            nc.vector.tensor_copy(
                out=wq_s[g][:].rearrange("p (r m) -> p r m", r=4),
                in_=wq_raw_s[:, 512 * g : 512 * (g + 1)].rearrange("p (m r) -> p r m", r=4),
            )

        turned = {}
        a_part = {}
        em_turned = {}
        product = {}
        acc = {}

        def turn(matrix, g, u, halves=(0, 1)):
            for h in halves:
                tile = bank((BANK_A if matrix == "a" else BANK_B) + h, "turned_%s%d%d%d" % (matrix, g, u, h))
                for i, b in enumerate(b for b in TURNED if b // 2 == h):
                    for e in range(2):
                        c = 256 * i + P * e
                        nc.tensor.transpose(tile[:, c : c + P], loaded[matrix, g, u, h][:, e, P * i : P * (i + 1)], ident[:])
                    turned[matrix, g, u, b] = tile[:, 256 * i : 256 * (i + 1)].rearrange("q (e p) -> q p e", e=2)

        def scale_a(g, u, blocks=TURNED):
            for b in blocks:
                tile = sbuf("a_part%d%d%d" % (g, u, b), [P, 256], F32)
                a_part[g, u, b] = tile[:].rearrange("q (p e) -> q p e", e=2)
                nc.scalar.activation(out=a_part[g, u, b], in_=turned["a", g, u, b], func=COPY, scale=sh_col[:, b : b + 1])

        def blend(g, u, blocks=TURNED):
            for b in blocks:
                tile = sbuf("em_turned%d%d%d" % (g, u, b), [P, 256], BF16)
                em_turned[g, u, b] = tile
                nc.vector.scalar_tensor_tensor(
                    out=tile[:].rearrange("q (p e) -> q p e", e=2),
                    in0=turned["b", g, u, b],
                    scalar=rest_col[:, b : b + 1],
                    in1=a_part[g, u, b],
                    op0=ALU.mult,
                    op1=ALU.add,
                )

        def turn_back_and_group(g, first, count, index):
            tile = bank(index, "back%d%d" % (g, first))
            for i in range(count):
                for u in range(2):
                    c = P * (u * count + i)
                    nc.tensor.transpose(tile[:, c : c + P], em_turned[g, u, first + i][:].bitcast(F32), ident[:])
            words = em_grouped[g][:].bitcast(F32).rearrange("p (r m u) -> p r m u", r=4, u=2)
            nc.scalar.copy(
                out=words[:, :, 32 * first : 32 * (first + count), :],
                in_=tile[:, 0 : 256 * count].rearrange("p (u m r) -> p r m u", u=2, r=4),
            )

        def multiply_as_loaded(matrix, g, u):
            tile = sbuf("product_%s%d%d" % (matrix, g, u), [P, 2, P], F32)
            product[matrix, g, u] = tile[:].rearrange("p e n -> p (e n)")
            share = sh_row if matrix == "a" else rest_row
            nc.vector.tensor_tensor(
                out=tile[:],
                in0=loaded[matrix, g, u, 1][:, :, P : 2 * P],
                in1=share[:].unsqueeze(1).broadcast_to([P, 2, P]),
                op=ALU.mult,
            )

        def add_as_loaded(g, u):
            nc.vector.tensor_tensor(
                out=em_as_loaded[g][:, 256 * u : 256 * (u + 1)], in0=product["a", g, u], in1=product["b", g, u], op=ALU.add
            )

        def group_as_loaded(g):
            nc.vector.tensor_copy(
                out=em_grouped[g][:].rearrange("p (r m j) -> p r m j", r=4, j=4)[:, :, 96:128, :],
                in_=em_as_loaded[g][:].rearrange("p (j m r) -> p r m j", j=4, r=4),
            )

        def quantise_em(g, first, count):
            nc.vector.quantize_mx(
                out=em_w[g][:, P * first : P * (first + count)].bitcast(FP8X4),
                scales=em_s[g][:, P * first : P * (first + count)],
                in_=em_grouped[g][:, 512 * first : 512 * (first + count)],
            )

        def given_pass(g, tiles):
            for r in tiles:
                if g == 0:
                    acc[r] = bank(BANK_OUT + r, "acc%d" % r)
                nc.tensor.matmul_mx(
                    out=acc[r][:],
                    lhsT=wq_w[g][:, 256 * r : 256 * (r + 1)].bitcast(FP4X4),
                    lhsT_scale=wq_s[g][:, P * r : P * (r + 1)],
                    rhs=xq_w[g][:].bitcast(FP8X4),
                    rhs_scale=xq_s[:, 512 * g : 512 * (g + 1)],
                    start=(g == 0),
                    stop=False,
                )

        def blended_pass(g, tiles):
            for r in tiles:
                nc.tensor.matmul_mx(
                    out=acc[r][:],
                    lhsT=em_w[g][:, P * r : P * (r + 1)].bitcast(FP8X4),
                    lhsT_scale=em_s[g][:, P * r : P * (r + 1)],
                    rhs=xt_w[g][:].bitcast(FP4X4),
                    rhs_scale=xt_s[:, 512 * g : 512 * (g + 1)],
                    start=False,
                    stop=(g == 1),
                )

        columns = bank(BANK_B, "columns")
        nc.tensor.transpose(columns[:, 0:P], sh_blocks[:], ident[:])
        nc.scalar.activation(out=rest_col[:], in_=columns[:, 0:4], func=COPY, scale=-1.0, bias=1.0)
        nc.scalar.copy(out=sh_col[:], in_=columns[:, 0:4])
        spread = bank(BANK_B + 1, "spread")
        nc.tensor.transpose(spread[:, 0:P], sh_col[:, 3:4].to_broadcast([P, P]), ident[:])
        nc.scalar.copy(out=sh_row[:], in_=spread[:, 0:P])
        nc.scalar.activation(out=rest_row[:], in_=spread[:, 0:P], func=COPY, scale=-1.0, bias=1.0)

        deal_words(0)
        deal_scales(0)
        turn("a", 0, 0)
        scale_a(0, 0)
        multiply_as_loaded("a", 0, 0)
        deal_words(1)
        turn("b", 0, 0)
        multiply_as_loaded("b", 0, 0)
        blend(0, 0)
        add_as_loaded(0, 0)
        deal_scales(1)
        given_pass(0, (0, 1))

        turn("a", 0, 1)
        scale_a(0, 1)
        multiply_as_loaded("a", 0, 1)
        given_pass(0, (2,))
        turn("b", 0, 1)
        multiply_as_loaded("b", 0, 1)
        blend(0, 1)
        add_as_loaded(0, 1)
        given_pass(1, (0, 1))

        turn_back_and_group(0, 0, 2, BANK_B)
        turn("a", 1, 0)
        scale_a(1, 0, (0,))
        turn_back_and_group(0, 2, 1, BANK_SPARE)
        scale_a(1, 0, (1, 2))
        group_as_loaded(0)
        multiply_as_loaded("a", 1, 0)
        given_pass(1, (2,))
        turn("b", 1, 0)
        multiply_as_loaded("b", 1, 0)
        quantise_em(0, 0, 4)
        blend(1, 0)
        add_as_loaded(1, 0)
        given_pass(0, (3,))
        given_pass(1, (3,))

        turn("a", 1, 1)
        scale_a(1, 1)
        multiply_as_loaded("a", 1, 1)
        turn("b", 1, 1, (0,))
        blend(1, 1, (0, 1))
        turn("b", 1, 1, (1,))
        multiply_as_loaded("b", 1, 1)
        blend(1, 1, (2,))
        add_as_loaded(1, 1)
        group_as_loaded(1)
        turn_back_and_group(1, 0, 1, BANK_A)
        turn_back_and_group(1, 1, 1, BANK_A + 1)
        blended_pass(0, (0,))
        turn_back_and_group(1, 2, 1, BANK_B)
        blended_pass(0, (1, 2))
        for r in range(4):
            quantise_em(1, r, 1)
        blended_pass(1, (0, 1, 2))
        blended_pass(0, (3,))
        blended_pass(1, (3,))

        y = sbuf("y", [P, 4, T], F32)
        y_grouped = [sbuf("y_grouped%d" % h, [P, 1024], BF16) for h in range(2)]
        y_w = sbuf("y_w", [P, T], U32)
        y_s = sbuf("y_s", [P, T], U8)
        out_rows = out_0.rearrange("(p r) t -> p r t", r=4)
        for c in (0, 256):
            nc.vector.tensor_copy(out=y[:, 0, c : c + 256], in_=acc[0][:, c : c + 256])
            nc.sync.dma_start(out=out_rows[:, 0, c : c + 256], in_=y[:, 0, c : c + 256])
        nc.scalar.copy(out=y[:, 1, :], in_=acc[1][:])
        nc.sync.dma_start(out=out_rows[:, 1, :], in_=y[:, 1, :])
        nc.vector.tensor_copy(out=y[:, 2, :], in_=acc[2][:])
        nc.sync.dma_start(out=out_rows[:, 2, :], in_=y[:, 2, :])
        nc.scalar.copy(out=y[:, 3, 0:256], in_=acc[3][:, 0:256])
        nc.scalar.copy(out=y[:, 3, 256:512], in_=acc[3][:, 256:512])
        nc.sync.dma_start(out=out_rows[:, 3, :], in_=y[:, 3, :])

        def group_result(copy, h, first, last):
            copy(
                out=y_grouped[h][:, 4 * first : 4 * last].rearrange("p (c i r) -> p c r i", i=4, r=4),
                in_=y[:, :, 256 * h + first : 256 * h + last].rearrange("p r (c i) -> p c r i", i=4),
            )

        group_result(nc.vector.tensor_copy, 0, 0, 256)
        group_result(nc.scalar.copy, 1, 0, SCALAR_COLUMNS)
        group_result(nc.vector.tensor_copy, 1, SCALAR_COLUMNS, 256)
        words_out = out_1[0].rearrange("p c j -> p (c j)").bitcast(I32)
        for h in range(2):
            tokens = slice(256 * h, 256 * (h + 1))
            nc.vector.quantize_mx(out=y_w[:, tokens].bitcast(FP8X4), scales=y_s[:, tokens], in_=y_grouped[h][:])
            nc.sync.dma_start(out=words_out[:, tokens], in_=y_w[:, tokens].bitcast(I32))
        for q in range(4):
            nc.scalar.dma_start(out=out_2[0].bitcast(I32)[4 * q : 4 * q + 4, :], in_=y_s[:].bitcast(I32)[32 * q : 32 * q + 4, :])
